import numpy as np
import ml_dtypes


def mxq(x, axis, fmt="e4m3"):
    dtype, down = {"e4m3": (ml_dtypes.float8_e4m3fn, 7), "e5m2": (ml_dtypes.float8_e5m2, 14)}[fmt]
    v = np.moveaxis(np.asarray(x, np.float32).astype(ml_dtypes.bfloat16).astype(np.float64), axis, -1)
    blocks = v.reshape(v.shape[:-1] + (-1, 32))
    amax = np.abs(blocks).max(-1, keepdims=True)
    byte = np.maximum(np.where(amax > 0, np.frexp(amax)[1] - 1 + 127, 0) - down, 1)
    scale = np.exp2(byte - 127.0)
    codes = (blocks / scale).astype(np.float32).astype(dtype).astype(np.float64)
    return np.moveaxis((codes * scale).reshape(v.shape), -1, axis)


WIDE = False


def mx_kscale(k):
    if not WIDE:
        return np.ones(k)
    levels = np.array([10, -10, 5, -5, 0])
    if k % 512:
        return np.exp2(np.random.permutation(np.resize(levels, k // 32))).repeat(32)
    a = np.empty((k // 512, 16))
    for p in range(k // 512):
        a[p, :8] = np.random.permutation(np.resize(levels, 8))
        for g in range(8):
            far = levels[np.abs(levels - a[p, g]) >= 10]
            a[p, g + 8] = far[np.random.randint(len(far))]
    return np.exp2(a.ravel()).repeat(32)


def f64(x):
    return np.asarray(x).astype(np.float64)


def striped8(idx):
    return np.asarray(idx).reshape(8, -1, 16).transpose(0, 2, 1).reshape(128, -1).astype(np.uint16)


def unstriped8(offs):
    return offs.reshape(8, 16, -1).transpose(0, 2, 1).reshape(8, -1).astype(np.int64)


def pick8(x, idx, run):
    r = np.arange(len(x))
    return x[r[:, None], idx[r % (8 * run) // run]]


E2M1 = np.array([0.0, 0.5, 1.0, 1.5, 2.0, 3.0, 4.0, 6.0, -0.0, -0.5, -1.0, -1.5, -2.0, -3.0, -4.0, -6.0])


def pack_weight(w, fmt):
    k, n = w.shape
    w = f64(np.asarray(w, np.float32).astype(ml_dtypes.bfloat16)).reshape(k // 32, 32, n)
    amax = np.abs(w).max(1)
    if fmt == "e4m3":
        byte = np.frexp(amax)[1] - 1 + 127 - 7
    else:
        mant, ex = np.frexp(amax / 6.0)
        byte = np.where(mant > 0.5, ex, ex - 1) + 127
    byte = np.clip(np.where(amax > 0, byte, 1), 1, 254)
    scaled = (w * np.exp2(127.0 - byte)[:, None, :]).reshape(k, n).astype(np.float32)
    by_word = np.ascontiguousarray(scaled.reshape(k // 512, 128, 4, n).transpose(0, 1, 3, 2))
    if fmt == "e4m3":
        words = by_word.astype(ml_dtypes.float8_e4m3fn).view(np.uint8)
    else:
        c = by_word.astype(ml_dtypes.float4_e2m1fn).view(np.uint8) & 0xF
        words = (c[..., 0::2] | (c[..., 1::2] << 4)).reshape(k // 512, 128, 2 * n)
    return np.ascontiguousarray(words), np.ascontiguousarray(byte.astype(np.uint8).reshape(k // 512, 16, n))


def unpack_weight(words, scales, fmt):
    g, _, n = scales.shape
    words = np.ascontiguousarray(words).reshape(g, 128, n, -1)
    if fmt == "e4m3":
        vals = words.view(ml_dtypes.float8_e4m3fn).astype(np.float64)
    else:
        nib = np.empty((g, 128, n, 4), np.uint8)
        nib[..., 0::2] = words & 0xF
        nib[..., 1::2] = words >> 4
        vals = E2M1[nib]
    vals = vals * np.repeat(np.exp2(scales.astype(np.float64) - 127.0), 8, axis=1)[..., None]
    return vals.transpose(0, 1, 3, 2).reshape(g * 512, n)


def sigmoid(v):
    return 1.0 / (1.0 + np.exp(-v))


def sgn(shape):
    return np.random.uniform(0.5, 2.0, shape) * np.where(np.random.standard_normal(shape) < 0, -1.0, 1.0)


D, K, T, U, X, I, Q = 512, 512, 1024, 1024, 1024, 512, 128


def setup_inputs():
    n = np.random.standard_normal
    idx = np.stack([np.random.permutation(X)[:I] for _ in range(8)])
    idx2 = np.stack([np.random.permutation(T)[:I] for _ in range(8)])
    idx3 = np.stack([np.random.permutation(T)[:I] for _ in range(8)])
    idx4 = np.stack([np.random.permutation(U)[:I] for _ in range(8)])
    idx5 = np.stack([np.random.permutation(T)[:I] for _ in range(8)])
    idx6 = np.stack([np.random.permutation(U)[:I] for _ in range(8)])
    fd = mx_kscale(D)
    fk = mx_kscale(K)
    wqp = pack_weight(n((D, K)) * 1.0 / np.sqrt(D) * fd[:, None] * fk, "e4m3")
    cachep = pack_weight(n((K, T)) * 1.0 / np.sqrt(K) / fk[:, None], "e4m3")
    draftp = pack_weight(n((K, U)) * 1.0 / np.sqrt(K) / fk[:, None], "e2m1")
    archp = pack_weight(n((D, X)) * 1.0 / np.sqrt(D) * fd[:, None], "e4m3")
    return {
        "states": (n((D, Q)) * 0.95 / fd[:, None]).astype(np.float32),
        "wq_words": wqp[0],
        "wq_scales": wqp[1],
        "cache_words": cachep[0],
        "cache_scales": cachep[1],
        "draft_words": draftp[0],
        "draft_scales": draftp[1],
        "arch_words": archp[0],
        "arch_scales": archp[1],
        "thr": (np.random.uniform(-2.0, 2.0, (Q, 1))).astype(np.float32),
        "slope": (sgn((Q, 1))).astype(np.float32),
        "offs": striped8(idx),
        "offs2": striped8(idx2),
        "offs3": striped8(idx3),
        "offs4": striped8(idx4),
        "offs5": striped8(idx5),
        "offs6": striped8(idx6),
    }


def reference(states, wq_words, wq_scales, cache_words, cache_scales, draft_words, draft_scales, arch_words, arch_scales, thr, slope, offs, offs2, offs3, offs4, offs5, offs6):
    idx = unstriped8(offs)
    idx2 = unstriped8(offs2)
    idx3 = unstriped8(offs3)
    idx4 = unstriped8(offs4)
    idx5 = unstriped8(offs5)
    idx6 = unstriped8(offs6)
    wqu = unpack_weight(wq_words, wq_scales, "e4m3")
    cacheu = unpack_weight(cache_words, cache_scales, "e4m3")
    draftu = unpack_weight(draft_words, draft_scales, "e2m1")
    archu = unpack_weight(arch_words, arch_scales, "e4m3")
    statesq = mxq(f64(states), 0, "e4m3")
    qv = wqu.T @ statesq
    qvq = mxq(qv, 0, "e4m3")
    a = qvq.T @ cacheu
    b = qvq.T @ draftu
    c0 = statesq.T @ archu
    s1 = sigmoid(pick8(c0, idx, 16) * f64(slope) + f64(thr))
    kp = np.zeros((Q, T))
    kp[np.arange(Q)[:, None], idx2[np.arange(Q) % 128 // 16]] = s1
    ev = a * kp
    aa = a - ev
    f1 = np.zeros((Q, U))
    f1[np.arange(Q)[:, None], idx4[np.arange(Q) % 128 // 16]] = pick8(ev, idx3, 16)
    bb = b + f1
    y = np.maximum(pick8(aa, idx5, 16), pick8(bb, idx6, 16))
    return y

@@ -1,0 +1,212 @@
+from contextlib import ExitStack
+
+import concourse.mybir as mybir
+from concourse.masks import make_identity
+
+F32 = mybir.dt.float32
+BF16 = mybir.dt.bfloat16
+I32 = mybir.dt.int32
+U32 = mybir.dt.uint32
+U16 = mybir.dt.uint16
+U8 = mybir.dt.uint8
+FP8X4 = mybir.dt.float8_e4m3fn_x4
+FP4X4 = mybir.dt.float4_e2m1fn_x4
+ALU = mybir.AluOpType
+ACT = mybir.ActivationFunctionType
+
+P = 128
+PACK = 4
+FEATURES = 512
+TOKENS = 1024
+SLOTS = 512
+BANK = 512
+GATE_PASS = 256
+LIST_COLS = SLOTS // 16
+POOL_COLS = 256
+
+FLOPS = 2 * P * FEATURES * (FEATURES + 3 * TOKENS)
+
+
+def tile_attend_fadeout_sidethree_kernel(
+    tc, states, wq_words, wq_scales, cache_words, cache_scales, draft_words, draft_scales,
+    arch_words, arch_scales, thr, slope, offs, offs2, offs3, offs4, offs5, offs6, out,
+):
+    nc = tc.nc
+    with ExitStack() as ctx:
+        sb = ctx.enter_context(tc.tile_pool(name="sb", bufs=1))
+        ps = ctx.enter_context(tc.psum_pool(name="ps", bufs=1))
+
+        def zeroed_plane(name, width):
+            plane = sb.tile([P, width], U8, name=name, align_bytes=64)
+            nc.vector.memset(plane[:].bitcast(I32), 0)
+            return plane
+
+        def load_plane(queue, plane, scales):
+            for r in range(4):
+                queue.dma_start(out=plane[:].bitcast(I32)[r:P:32, :], in_=scales[0].bitcast(I32)[r:16:4, :])
+
+        def load_packed_plane(queue, plane, scales, width):
+            for quad in range(4):
+                rows = scales[0].bitcast(I32)[4 * quad : 4 * quad + 4, :]
+                queue.dma_start(
+                    out=plane[:].bitcast(I32)[32 * quad : 32 * quad + 16, :],
+                    in_=rows.rearrange("j (c n) -> c j n", c=4),
+                )
+
+        def load_words(name, words, c0, c1):
+            tile = sb.tile([P, c1 - c0], U32, name=name, align_bytes=64)
+            flat = words[0].rearrange("p n t -> p (n t)")
+            nc.sync.dma_start(out=tile[:].bitcast(I32), in_=flat[:, PACK * c0 : PACK * c1].bitcast(I32))
+            return tile
+
+        def load_list(name, src):
+            tile = sb.tile([P, LIST_COLS], U16, name=name)
+            nc.sync.dma_start(tile[:], src)
+            return tile
+
+        def load_column(name, src):
+            tile = sb.tile([P, 1], F32, name=name)
+            nc.sync.dma_start(out=tile[:], in_=src)
+            return tile
+
+        arch_plane = zeroed_plane("arch_plane", GATE_PASS)
+        raw = sb.tile([P, PACK, P], F32, name="raw")
+        nc.sync.dma_start(out=raw[:], in_=states.rearrange("(p j) q -> p j q", j=PACK))
+        load_packed_plane(nc.scalar, arch_plane, arch_scales, GATE_PASS)
+        arch_w = load_words("arch_w", arch_words, 0, TOKENS)
+        list1 = load_list("list1", offs)
+        slope_t = load_column("slope_t", slope)
+        thr_t = load_column("thr_t", thr)
+
+        wq_plane = zeroed_plane("wq_plane", P)
+        cache_plane = zeroed_plane("cache_plane", GATE_PASS)
+        draft_plane = zeroed_plane("draft_plane", TOKENS)
+        list2 = load_list("list2", offs2)
+        wq_w = load_words("wq_w", wq_words, 0, FEATURES)
+        load_packed_plane(nc.sync, wq_plane, wq_scales, P)
+        cache_w = load_words("cache_w", cache_words, 0, TOKENS)
+        load_packed_plane(nc.sync, cache_plane, cache_scales, GATE_PASS)
+        list3 = load_list("list3", offs3)
+        list4 = load_list("list4", offs4)
+        draft_w = sb.tile([P, 2 * TOKENS], U8, name="draft_w", align_bytes=64)
+        nc.sync.dma_start(out=draft_w[:].bitcast(I32), in_=draft_words[0].bitcast(I32))
+        load_plane(nc.sync, draft_plane, draft_scales)
+        list5 = load_list("list5", offs5)
+        list6 = load_list("list6", offs6)
+
+        warm_in = sb.tile([P, 1], F32, name="warm_in")
+        nc.vector.memset(warm_in[:], 0.0)
+        warm_out = sb.tile([P, 1], F32, name="warm_out")
+        nc.scalar.activation(warm_out[:], warm_in[:], ACT.Sigmoid)
+
+        kp = sb.tile([P, TOKENS], F32, name="kp")
+        nc.vector.memset(kp[:], 0.0)
+        f1 = sb.tile([P, TOKENS], F32, name="f1")
+        nc.vector.memset(f1[:], 0.0)
+        ident = sb.tile([P, P], F32, name="ident")
+        make_identity(nc, ident[:])
+
+        st_bf = sb.tile([P, P, PACK], BF16, name="st_bf", align_bytes=64)
+        nc.vector.tensor_copy(
+            out=st_bf[:].rearrange("p (c i) j -> p c j i", i=4),
+            in_=raw[:].rearrange("p j (c i) -> p c j i", i=4),
+        )
+        st_w = sb.tile([P, P], U32, name="st_w", align_bytes=64)
+        st_plane = sb.tile([P, P], U8, name="st_plane", align_bytes=64)
+        nc.vector.quantize_mx(out=st_w[:].bitcast(FP8X4), scales=st_plane[:], in_=st_bf[:].rearrange("p q j -> p (q j)"))
+
+        c0 = sb.tile([P, TOKENS], F32, name="c0")
+        for g in range(TOKENS // GATE_PASS):
+            acc = ps.tile([P, GATE_PASS], F32, name="c0_ps%d" % g, tag="bank%d" % g)
+            lo = g * GATE_PASS
+            nc.tensor.matmul_mx(
+                out=acc[:], lhsT=st_w[:].bitcast(FP8X4), lhsT_scale=st_plane[:],
+                rhs=arch_w[:, lo : lo + GATE_PASS].bitcast(FP8X4),
+                rhs_scale=arch_plane[4 * g :, :], start=True, stop=True,
+            )
+            nc.vector.tensor_copy(out=c0[:, lo : lo + GATE_PASS], in_=acc[:])
+
+        s1 = sb.tile([P, SLOTS], F32, name="s1")
+        nc.scalar.activation(s1[:], c0[:].indirect(list1[:]), ACT.Sigmoid, bias=thr_t[:], scale=slope_t[:])
+        nc.scalar.activation(kp[:].indirect(list2[:]), s1[:], ACT.Copy)
+
+        qvT_ps = ps.tile([P, FEATURES], F32, name="qvT_ps", tag="bank4")
+        for g in range(4):
+            nc.tensor.matmul_mx(
+                out=qvT_ps[:, g * P : (g + 1) * P], lhsT=st_w[:].bitcast(FP8X4), lhsT_scale=st_plane[:],
+                rhs=wq_w[:, g * P : (g + 1) * P].bitcast(FP8X4), rhs_scale=wq_plane[4 * g :, :], start=True, stop=True,
+            )
+        qvT_bf = sb.tile([P, 2, P, 2], BF16, name="qvT_bf")
+        nc.vector.tensor_copy(out=qvT_bf[:], in_=qvT_ps[:].rearrange("q (p u e) -> q u p e", u=2, e=2))
+        qvT_pairs = qvT_bf[:].rearrange("q u p e -> q (u p e)").bitcast(F32)
+        turn_ps = ps.tile([P, 2, P], F32, name="turn_ps", tag="bank5")
+        for u in range(2):
+            nc.tensor.transpose(turn_ps[:, u, :], qvT_pairs[:, u * P : (u + 1) * P], ident[:])
+        qv_bf = sb.tile([P, P * PACK], BF16, name="qv_bf", align_bytes=64)
+        nc.vector.tensor_copy(
+            out=qv_bf[:].bitcast(F32).rearrange("p (q u) -> p q u", u=2),
+            in_=turn_ps[:].rearrange("p u q -> p q u"),
+        )
+        qv_w = sb.tile([P, P], U32, name="qv_w", align_bytes=64)
+        qv_plane = sb.tile([P, P], U8, name="qv_plane", align_bytes=64)
+        nc.vector.quantize_mx(out=qv_w[:].bitcast(FP8X4), scales=qv_plane[:], in_=qv_bf[:])
+
+        halves = [slice(h * BANK, (h + 1) * BANK) for h in range(2)]
+        def cache_pass(acc, g):
+            lo = g * GATE_PASS
+            nc.tensor.matmul_mx(
+                out=acc, lhsT=qv_w[:].bitcast(FP8X4), lhsT_scale=qv_plane[:],
+                rhs=cache_w[:, lo : lo + GATE_PASS].bitcast(FP8X4), rhs_scale=cache_plane[4 * g :, :],
+                start=True, stop=True,
+            )
+
+        def draft_pass(acc, lo, hi):
+            nc.tensor.matmul_mx(
+                out=acc, lhsT=qv_w[:].bitcast(FP8X4), lhsT_scale=qv_plane[:],
+                rhs=draft_w[:, 2 * lo : 2 * hi].bitcast(FP4X4),
+                rhs_scale=draft_plane[:, lo:hi], start=True, stop=True,
+            )
+
+        a_ps = [ps.tile([P, BANK], F32, name="a_ps%d" % h, tag="bank%d" % (6 + h)) for h in range(2)]
+        for g in (2, 3, 0, 1):
+            lo = (g % 2) * GATE_PASS
+            cache_pass(a_ps[g // 2][:, lo : lo + GATE_PASS], g)
+        b_ps = [ps.tile([P, BANK], F32, name="b_ps%d" % h, tag="bank%d" % h) for h in range(2)]
+        for h in (1, 0):
+            draft_pass(b_ps[h][:], h * BANK, (h + 1) * BANK)
+
+        cut = TOKENS - POOL_COLS
+        a_tail = sb.tile([P, POOL_COLS], F32, name="a_tail", tag="tail")
+        nc.vector.tensor_copy(out=a_tail[:], in_=a_ps[1][:, cut - BANK :])
+        ev = sb.tile([P, TOKENS], F32, name="ev", tag="cached_scores")
+        nc.gpsimd.tensor_tensor(ev[:, cut:], a_tail[:], kp[:, cut:], ALU.mult)
+        nc.vector.tensor_tensor(ev[:, :BANK], a_ps[0][:], kp[:, :BANK], ALU.mult)
+        nc.vector.tensor_tensor(ev[:, BANK:cut], a_ps[1][:, : cut - BANK], kp[:, BANK:cut], ALU.mult)
+
+        half_slots = SLOTS // 2
+        half_cols = LIST_COLS // 2
+        moved = sb.tile([P, SLOTS], F32, name="moved")
+        nc.vector.tensor_copy(moved[:, :half_slots], ev[:].indirect(list3[:, :half_cols]))
+        nc.scalar.activation(moved[:, half_slots:], ev[:].indirect(list3[:, half_cols:]), ACT.Copy)
+        nc.scalar.activation(f1[:].indirect(list4[:]), moved[:], ACT.Copy)
+
+        aa = ev
+        for h in range(2):
+            nc.vector.tensor_tensor(aa[:, halves[h]], a_ps[h][:], ev[:, halves[h]], ALU.subtract)
+        left = sb.tile([P, SLOTS], F32, name="left")
+        nc.vector.tensor_copy(left[:], aa[:].indirect(list5[:]))
+
+        bb = sb.tile([P, TOKENS], F32, name="bb", tag="cached_scores")
+        b_tail = sb.tile([P, POOL_COLS], F32, name="b_tail", tag="tail")
+        nc.vector.tensor_copy(out=b_tail[:], in_=b_ps[1][:, cut - BANK :])
+        nc.gpsimd.tensor_tensor(bb[:, cut:], b_tail[:], f1[:, cut:], ALU.add)
+        nc.vector.tensor_tensor(bb[:, :BANK], b_ps[0][:], f1[:, :BANK], ALU.add)
+        nc.vector.tensor_tensor(bb[:, BANK:cut], b_ps[1][:, : cut - BANK], f1[:, BANK:cut], ALU.add)
+        stood = sb.tile([P, SLOTS], F32, name="stood")
+        nc.vector.tensor_copy(stood[:, :half_slots], bb[:].indirect(list6[:, :half_cols]))
+        nc.scalar.activation(stood[:, half_slots:], bb[:].indirect(list6[:, half_cols:]), ACT.Copy)
+        y = sb.tile([P, SLOTS], F32, name="y")
+        for h, queue in enumerate((nc.scalar, nc.sync)):
+            cols = slice(h * half_slots, (h + 1) * half_slots)
+            nc.vector.tensor_tensor(y[:, cols], left[:, cols], stood[:, cols], ALU.max)
+            queue.dma_start(out=out[:, cols], in_=y[:, cols])

@@ -94,11 +94,6 @@ def tile_attend_fadeout_sidethree_kernel(
         list5 = load_list("list5", offs5)
         list6 = load_list("list6", offs6)
 
-        warm_in = sb.tile([P, 1], F32, name="warm_in")
-        nc.vector.memset(warm_in[:], 0.0)
-        warm_out = sb.tile([P, 1], F32, name="warm_out")
-        nc.scalar.activation(warm_out[:], warm_in[:], ACT.Sigmoid)
-
         kp = sb.tile([P, TOKENS], F32, name="kp")
         nc.vector.memset(kp[:], 0.0)
         f1 = sb.tile([P, TOKENS], F32, name="f1")

@@ -22,7 +22,7 @@ SLOTS = 512
 BANK = 512
 GATE_PASS = 256
 LIST_COLS = SLOTS // 16
-POOL_COLS = 256
+POOL_COLS = 336
 
 FLOPS = 2 * P * FEATURES * (FEATURES + 3 * TOKENS)
 
@@ -64,26 +64,26 @@ def tile_attend_fadeout_sidethree_kernel(
             nc.sync.dma_start(tile[:], src)
             return tile
 
-        def load_column(name, src):
+        def load_column(queue, name, src):
             tile = sb.tile([P, 1], F32, name=name)
-            nc.sync.dma_start(out=tile[:], in_=src)
+            queue.dma_start(out=tile[:], in_=src)
             return tile
 
+        slope_t = load_column(nc.scalar, "slope_t", slope)
         arch_plane = zeroed_plane("arch_plane", GATE_PASS)
         raw = sb.tile([P, PACK, P], F32, name="raw")
         nc.sync.dma_start(out=raw[:], in_=states.rearrange("(p j) q -> p j q", j=PACK))
         load_packed_plane(nc.scalar, arch_plane, arch_scales, GATE_PASS)
         arch_w = load_words("arch_w", arch_words, 0, TOKENS)
         list1 = load_list("list1", offs)
-        slope_t = load_column("slope_t", slope)
-        thr_t = load_column("thr_t", thr)
+        thr_t = load_column(nc.sync, "thr_t", thr)
 
         wq_plane = zeroed_plane("wq_plane", P)
         cache_plane = zeroed_plane("cache_plane", GATE_PASS)
         draft_plane = zeroed_plane("draft_plane", TOKENS)
-        list2 = load_list("list2", offs2)
         wq_w = load_words("wq_w", wq_words, 0, FEATURES)
         load_packed_plane(nc.sync, wq_plane, wq_scales, P)
+        list2 = load_list("list2", offs2)
         cache_w = load_words("cache_w", cache_words, 0, TOKENS)
         load_packed_plane(nc.sync, cache_plane, cache_scales, GATE_PASS)
         list3 = load_list("list3", offs3)
@@ -131,12 +131,12 @@ def tile_attend_fadeout_sidethree_kernel(
                 out=qvT_ps[:, g * P : (g + 1) * P], lhsT=st_w[:].bitcast(FP8X4), lhsT_scale=st_plane[:],
                 rhs=wq_w[:, g * P : (g + 1) * P].bitcast(FP8X4), rhs_scale=wq_plane[4 * g :, :], start=True, stop=True,
             )
-        qvT_bf = sb.tile([P, 2, P, 2], BF16, name="qvT_bf")
-        nc.vector.tensor_copy(out=qvT_bf[:], in_=qvT_ps[:].rearrange("q (p u e) -> q u p e", u=2, e=2))
-        qvT_pairs = qvT_bf[:].rearrange("q u p e -> q (u p e)").bitcast(F32)
+        qvT_bf = [sb.tile([P, P, 2], BF16, name="qvT_bf%d" % u) for u in range(2)]
+        for u in range(2):
+            nc.vector.tensor_copy(out=qvT_bf[u][:], in_=qvT_ps[:].rearrange("q (p u e) -> q u p e", u=2, e=2)[:, u])
         turn_ps = ps.tile([P, 2, P], F32, name="turn_ps", tag="bank5")
         for u in range(2):
-            nc.tensor.transpose(turn_ps[:, u, :], qvT_pairs[:, u * P : (u + 1) * P], ident[:])
+            nc.tensor.transpose(turn_ps[:, u, :], qvT_bf[u][:].rearrange("q p e -> q (p e)").bitcast(F32), ident[:])
         qv_bf = sb.tile([P, P * PACK], BF16, name="qv_bf", align_bytes=64)
         nc.vector.tensor_copy(
             out=qv_bf[:].bitcast(F32).rearrange("p (q u) -> p q u", u=2),

@@ -94,6 +94,11 @@ def tile_attend_fadeout_sidethree_kernel(
         list5 = load_list("list5", offs5)
         list6 = load_list("list6", offs6)
 
+        warm_in = sb.tile([P, 1], F32, name="warm_in")
+        nc.vector.memset(warm_in[:], 0.0)
+        warm_out = sb.tile([P, 1], F32, name="warm_out")
+        nc.scalar.activation(warm_out[:], warm_in[:], ACT.Sigmoid)
+
         kp = sb.tile([P, TOKENS], F32, name="kp")
         nc.vector.memset(kp[:], 0.0)
         f1 = sb.tile([P, TOKENS], F32, name="f1")

from contextlib import ExitStack

import concourse.mybir as mybir
from concourse.masks import make_identity

F32 = mybir.dt.float32
BF16 = mybir.dt.bfloat16
I32 = mybir.dt.int32
U32 = mybir.dt.uint32
U16 = mybir.dt.uint16
U8 = mybir.dt.uint8
FP8X4 = mybir.dt.float8_e4m3fn_x4
FP4X4 = mybir.dt.float4_e2m1fn_x4
ALU = mybir.AluOpType
ACT = mybir.ActivationFunctionType

P = 128
PACK = 4
FEATURES = 512
TOKENS = 1024
SLOTS = 512
BANK = 512
GATE_PASS = 256
LIST_COLS = SLOTS // 16
POOL_COLS = 336

FLOPS = 2 * P * FEATURES * (FEATURES + 3 * TOKENS)


def tile_attend_fadeout_sidethree_kernel(
    tc, states, wq_words, wq_scales, cache_words, cache_scales, draft_words, draft_scales,
    arch_words, arch_scales, thr, slope, offs, offs2, offs3, offs4, offs5, offs6, out,
):
    nc = tc.nc
    with ExitStack() as ctx:
        sb = ctx.enter_context(tc.tile_pool(name="sb", bufs=1))
        ps = ctx.enter_context(tc.psum_pool(name="ps", bufs=1))

        def zeroed_plane(name, width):
            plane = sb.tile([P, width], U8, name=name, align_bytes=64)
            nc.vector.memset(plane[:].bitcast(I32), 0)
            return plane

        def load_plane(queue, plane, scales):
            for r in range(4):
                queue.dma_start(out=plane[:].bitcast(I32)[r:P:32, :], in_=scales[0].bitcast(I32)[r:16:4, :])

        def load_packed_plane(queue, plane, scales, width):
            for quad in range(4):
                rows = scales[0].bitcast(I32)[4 * quad : 4 * quad + 4, :]
                queue.dma_start(
                    out=plane[:].bitcast(I32)[32 * quad : 32 * quad + 16, :],
                    in_=rows.rearrange("j (c n) -> c j n", c=4),
                )

        def load_words(name, words, c0, c1):
            tile = sb.tile([P, c1 - c0], U32, name=name, align_bytes=64)
            flat = words[0].rearrange("p n t -> p (n t)")
            nc.sync.dma_start(out=tile[:].bitcast(I32), in_=flat[:, PACK * c0 : PACK * c1].bitcast(I32))
            return tile

        def load_list(name, src):
            tile = sb.tile([P, LIST_COLS], U16, name=name)
            nc.sync.dma_start(tile[:], src)
            return tile

        def load_column(queue, name, src):
            tile = sb.tile([P, 1], F32, name=name)
            queue.dma_start(out=tile[:], in_=src)
            return tile

        slope_t = load_column(nc.scalar, "slope_t", slope)
        arch_plane = zeroed_plane("arch_plane", GATE_PASS)
        raw = sb.tile([P, PACK, P], F32, name="raw")
        nc.sync.dma_start(out=raw[:], in_=states.rearrange("(p j) q -> p j q", j=PACK))
        load_packed_plane(nc.scalar, arch_plane, arch_scales, GATE_PASS)
        arch_w = load_words("arch_w", arch_words, 0, TOKENS)
        list1 = load_list("list1", offs)
        thr_t = load_column(nc.sync, "thr_t", thr)

        wq_plane = zeroed_plane("wq_plane", P)
        cache_plane = zeroed_plane("cache_plane", GATE_PASS)
        draft_plane = zeroed_plane("draft_plane", TOKENS)
        wq_w = load_words("wq_w", wq_words, 0, FEATURES)
        load_packed_plane(nc.sync, wq_plane, wq_scales, P)
        list2 = load_list("list2", offs2)
        cache_w = load_words("cache_w", cache_words, 0, TOKENS)
        load_packed_plane(nc.sync, cache_plane, cache_scales, GATE_PASS)
        list3 = load_list("list3", offs3)
        list4 = load_list("list4", offs4)
        draft_w = sb.tile([P, 2 * TOKENS], U8, name="draft_w", align_bytes=64)
        nc.sync.dma_start(out=draft_w[:].bitcast(I32), in_=draft_words[0].bitcast(I32))
        load_plane(nc.sync, draft_plane, draft_scales)
        list5 = load_list("list5", offs5)
        list6 = load_list("list6", offs6)

        warm_in = sb.tile([P, 1], F32, name="warm_in")
        nc.vector.memset(warm_in[:], 0.0)
        warm_out = sb.tile([P, 1], F32, name="warm_out")
        nc.scalar.activation(warm_out[:], warm_in[:], ACT.Sigmoid)

        kp = sb.tile([P, TOKENS], F32, name="kp")
        nc.vector.memset(kp[:], 0.0)
        f1 = sb.tile([P, TOKENS], F32, name="f1")
        nc.vector.memset(f1[:], 0.0)
        ident = sb.tile([P, P], F32, name="ident")
        make_identity(nc, ident[:])

        st_bf = sb.tile([P, P, PACK], BF16, name="st_bf", align_bytes=64)
        nc.vector.tensor_copy(
            out=st_bf[:].rearrange("p (c i) j -> p c j i", i=4),
            in_=raw[:].rearrange("p j (c i) -> p c j i", i=4),
        )
        st_w = sb.tile([P, P], U32, name="st_w", align_bytes=64)
        st_plane = sb.tile([P, P], U8, name="st_plane", align_bytes=64)
        nc.vector.quantize_mx(out=st_w[:].bitcast(FP8X4), scales=st_plane[:], in_=st_bf[:].rearrange("p q j -> p (q j)"))

        c0 = sb.tile([P, TOKENS], F32, name="c0")
        for g in range(TOKENS // GATE_PASS):
            acc = ps.tile([P, GATE_PASS], F32, name="c0_ps%d" % g, tag="bank%d" % g)
            lo = g * GATE_PASS
            nc.tensor.matmul_mx(
                out=acc[:], lhsT=st_w[:].bitcast(FP8X4), lhsT_scale=st_plane[:],
                rhs=arch_w[:, lo : lo + GATE_PASS].bitcast(FP8X4),
                rhs_scale=arch_plane[4 * g :, :], start=True, stop=True,
            )
            nc.vector.tensor_copy(out=c0[:, lo : lo + GATE_PASS], in_=acc[:])

        s1 = sb.tile([P, SLOTS], F32, name="s1")
        nc.scalar.activation(s1[:], c0[:].indirect(list1[:]), ACT.Sigmoid, bias=thr_t[:], scale=slope_t[:])
        nc.scalar.activation(kp[:].indirect(list2[:]), s1[:], ACT.Copy)

        qvT_ps = ps.tile([P, FEATURES], F32, name="qvT_ps", tag="bank4")
        for g in range(4):
            nc.tensor.matmul_mx(
                out=qvT_ps[:, g * P : (g + 1) * P], lhsT=st_w[:].bitcast(FP8X4), lhsT_scale=st_plane[:],
                rhs=wq_w[:, g * P : (g + 1) * P].bitcast(FP8X4), rhs_scale=wq_plane[4 * g :, :], start=True, stop=True,
            )
        qvT_bf = [sb.tile([P, P, 2], BF16, name="qvT_bf%d" % u) for u in range(2)]
        for u in range(2):
            nc.vector.tensor_copy(out=qvT_bf[u][:], in_=qvT_ps[:].rearrange("q (p u e) -> q u p e", u=2, e=2)[:, u])
        turn_ps = ps.tile([P, 2, P], F32, name="turn_ps", tag="bank5")
        for u in range(2):
            nc.tensor.transpose(turn_ps[:, u, :], qvT_bf[u][:].rearrange("q p e -> q (p e)").bitcast(F32), ident[:])
        qv_bf = sb.tile([P, P * PACK], BF16, name="qv_bf", align_bytes=64)
        nc.vector.tensor_copy(
            out=qv_bf[:].bitcast(F32).rearrange("p (q u) -> p q u", u=2),
            in_=turn_ps[:].rearrange("p u q -> p q u"),
        )
        qv_w = sb.tile([P, P], U32, name="qv_w", align_bytes=64)
        qv_plane = sb.tile([P, P], U8, name="qv_plane", align_bytes=64)
        nc.vector.quantize_mx(out=qv_w[:].bitcast(FP8X4), scales=qv_plane[:], in_=qv_bf[:])

        halves = [slice(h * BANK, (h + 1) * BANK) for h in range(2)]
        def cache_pass(acc, g):
            lo = g * GATE_PASS
            nc.tensor.matmul_mx(
                out=acc, lhsT=qv_w[:].bitcast(FP8X4), lhsT_scale=qv_plane[:],
                rhs=cache_w[:, lo : lo + GATE_PASS].bitcast(FP8X4), rhs_scale=cache_plane[4 * g :, :],
                start=True, stop=True,
            )

        def draft_pass(acc, lo, hi):
            nc.tensor.matmul_mx(
                out=acc, lhsT=qv_w[:].bitcast(FP8X4), lhsT_scale=qv_plane[:],
                rhs=draft_w[:, 2 * lo : 2 * hi].bitcast(FP4X4),
                rhs_scale=draft_plane[:, lo:hi], start=True, stop=True,
            )

        a_ps = [ps.tile([P, BANK], F32, name="a_ps%d" % h, tag="bank%d" % (6 + h)) for h in range(2)]
        for g in (2, 3, 0, 1):
            lo = (g % 2) * GATE_PASS
            cache_pass(a_ps[g // 2][:, lo : lo + GATE_PASS], g)
        b_ps = [ps.tile([P, BANK], F32, name="b_ps%d" % h, tag="bank%d" % h) for h in range(2)]
        for h in (1, 0):
            draft_pass(b_ps[h][:], h * BANK, (h + 1) * BANK)

        cut = TOKENS - POOL_COLS
        a_tail = sb.tile([P, POOL_COLS], F32, name="a_tail", tag="tail")
        nc.vector.tensor_copy(out=a_tail[:], in_=a_ps[1][:, cut - BANK :])
        ev = sb.tile([P, TOKENS], F32, name="ev", tag="cached_scores")
        nc.gpsimd.tensor_tensor(ev[:, cut:], a_tail[:], kp[:, cut:], ALU.mult)
        nc.vector.tensor_tensor(ev[:, :BANK], a_ps[0][:], kp[:, :BANK], ALU.mult)
        nc.vector.tensor_tensor(ev[:, BANK:cut], a_ps[1][:, : cut - BANK], kp[:, BANK:cut], ALU.mult)

        half_slots = SLOTS // 2
        half_cols = LIST_COLS // 2
        moved = sb.tile([P, SLOTS], F32, name="moved")
        nc.vector.tensor_copy(moved[:, :half_slots], ev[:].indirect(list3[:, :half_cols]))
        nc.scalar.activation(moved[:, half_slots:], ev[:].indirect(list3[:, half_cols:]), ACT.Copy)
        nc.scalar.activation(f1[:].indirect(list4[:]), moved[:], ACT.Copy)

        aa = ev
        for h in range(2):
            nc.vector.tensor_tensor(aa[:, halves[h]], a_ps[h][:], ev[:, halves[h]], ALU.subtract)
        left = sb.tile([P, SLOTS], F32, name="left")
        nc.vector.tensor_copy(left[:], aa[:].indirect(list5[:]))

        bb = sb.tile([P, TOKENS], F32, name="bb", tag="cached_scores")
        b_tail = sb.tile([P, POOL_COLS], F32, name="b_tail", tag="tail")
        nc.vector.tensor_copy(out=b_tail[:], in_=b_ps[1][:, cut - BANK :])
        nc.gpsimd.tensor_tensor(bb[:, cut:], b_tail[:], f1[:, cut:], ALU.add)
        nc.vector.tensor_tensor(bb[:, :BANK], b_ps[0][:], f1[:, :BANK], ALU.add)
        nc.vector.tensor_tensor(bb[:, BANK:cut], b_ps[1][:, : cut - BANK], f1[:, BANK:cut], ALU.add)
        stood = sb.tile([P, SLOTS], F32, name="stood")
        nc.vector.tensor_copy(stood[:, :half_slots], bb[:].indirect(list6[:, :half_cols]))
        nc.scalar.activation(stood[:, half_slots:], bb[:].indirect(list6[:, half_cols:]), ACT.Copy)
        y = sb.tile([P, SLOTS], F32, name="y")
        for h, queue in enumerate((nc.scalar, nc.sync)):
            cols = slice(h * half_slots, (h + 1) * half_slots)
            nc.vector.tensor_tensor(y[:, cols], left[:, cols], stood[:, cols], ALU.max)
            queue.dma_start(out=out[:, cols], in_=y[:, cols])
